import numpy as np
CORES = [8,9,10,11,12,13,14,15,136,137,138,139,140,141,142,143]
N = 16
ROOT = 12
def setup_inputs(rng):
    return {"x": rng.standard_normal((N, 128, 2048), dtype=np.float32)}
def reference(x):
    y = np.full(x.shape, np.nan, x.dtype)
    y[ROOT] = x.sum(axis=0, dtype=np.float64).astype(x.dtype)
    return {"y": y}

@@ -1,0 +1,88 @@
+from concourse.bass import DstId, RemoteDMATransfer
+K = 4
+R = 128 // K
+W = 2 * R
+NS = 15
+SCRATCH = {'xs': ('dram', [8 * K, 128, W], 'float32'), 'rb': ('dram', [NS * K, 128, W], 'float32')}
+SEMAPHORES = ['ld0', 'ld1', 'ld2', 'ld3', 'arr0', 'arr1', 'arr2', 'arr3', 'sent', 'fin']
+
+def rank_program(g, core, T, topo):
+    if T.rank_of(core) is None:
+        return
+    LD = [T.sem.ld0, T.sem.ld1, T.sem.ld2, T.sem.ld3]
+    ARR = [T.sem.arr0, T.sem.arr1, T.sem.arr2, T.sem.arr3]
+    root = T.cores[12]
+    rl = root % 8
+    hb = root - rl
+    ha = min((c - c % 8 for c in T.cores if c - c % 8 != hb))
+    loc = core % 8
+    on_a = core - loc == ha
+
+    def owner_a(k, s):
+        if s // 4 == rl // 4:
+            return ha + 4 * (s // 4) + (s % 4 + k) % 4
+        return ha + s
+
+    def dst_id(d):
+        rid, pid = topo.addr(d, core)
+        return DstId(rid=rid, pnc=pid)
+
+    def plan(q):
+        ql, qa = (q % 8, q - q % 8 == ha)
+        pieces = []
+        for k in range(K):
+            for s in range(8):
+                d = owner_a(k, s) if qa or s == rl else hb + s
+                if d == q:
+                    continue
+                if qa:
+                    idx = (ql - d % 8 - 1) % 8
+                elif s == rl:
+                    idx = 7 + ql
+                else:
+                    idx = [j for j in range(8) if j != d % 8].index(ql)
+                pieces.append((k, s, d, idx))
+        calls = []
+        for i in range(0, len(pieces), 8):
+            grp = pieces[i:i + 8]
+            ne = 16 // len(grp)
+            grp = sorted(grp, key=lambda p: p[2] - p[2] % 8 == q - ql)
+            calls.append([p + ((1 << ne) - 1 << ne * j, ne) for j, p in enumerate(grp)])
+        return calls
+    lands = [0] * K
+    for q in T.cores:
+        if q != core:
+            for call in plan(q):
+                for k, s, d, idx, mask, ne in call:
+                    if d == core:
+                        lands[k] += ne
+    sent = 0
+    for k in range(K):
+        g.dma_start(T.xs[8 * k:8 * (k + 1)], T.x[R * k:R * (k + 1), :]).then_inc(LD[k], 16)
+    have = 0
+    for call in plan(core):
+        while have <= max((p[0] for p in call)):
+            g.wait_ge(LD[have], 16)
+            have += 1
+        g.remote_dma_fused([RemoteDMATransfer(dst_ids=[dst_id(d)], dma_engine_mask=mask, remote_sem=ARR[k], src=T.xs[8 * k + s], dst=T.rb[NS * k + idx]) for k, s, d, idx, mask, ne in call], local_sem=T.sem.sent)
+        sent += 16
+    if core == root:
+        for k in range(K):
+            g.wait_ge(ARR[k], 7 * 16 + 8)
+            g.dma_start(T.y[R * k:R * (k + 1), :], T.rb[NS * k:NS * k + 8]).then_inc(T.sem.fin, 16)
+        g.wait_ge(T.sem.fin, 16 * K)
+        g.wait_ge(T.sem.sent, sent)
+        return
+    for k in range(K):
+        if on_a:
+            s = [t for t in range(8) if owner_a(k, t) == core][0]
+            n = 15 if s == rl else 7
+            g.wait_ge(ARR[k], lands[k])
+            d, out, mask, ne = (root, T.rb[NS * k + s], 255, 8) if s == rl else (hb + s, T.rb[NS * k + 7], 255, 8)
+        else:
+            s, n = (loc, 8)
+            g.wait_ge(ARR[k], lands[k] + 8)
+            d, out, mask, ne = (root, T.rb[NS * k + s], 65535, 16)
+        g.remote_dma_fused([RemoteDMATransfer(dst_ids=[dst_id(d)], dma_engine_mask=mask, remote_sem=ARR[k], srcs=[T.xs[8 * k + s]] + [T.rb[NS * k + i] for i in range(n)], dsts=[out], alu_op=1)], local_sem=T.sem.sent)
+        sent += ne
+    g.wait_ge(T.sem.sent, sent)

@@ -4,13 +4,15 @@ R = 128 // K
 W = 2 * R
 NS = 15
 SCRATCH = {'xs': ('dram', [8 * K, 128, W], 'float32'), 'rb': ('dram', [NS * K, 128, W], 'float32')}
-SEMAPHORES = ['ld0', 'ld1', 'ld2', 'ld3', 'arr0', 'arr1', 'arr2', 'arr3', 'sent', 'fin']
+SEMAPHORES = ['ld0', 'ld1', 'ld2', 'ld3', 'ld4', 'ld5', 'ld6', 'ld7',
+              'arr0', 'arr1', 'arr2', 'arr3', 'arr4', 'arr5', 'arr6', 'arr7', 'sent', 'fin']
+
 
 def rank_program(g, core, T, topo):
     if T.rank_of(core) is None:
         return
-    LD = [T.sem.ld0, T.sem.ld1, T.sem.ld2, T.sem.ld3]
-    ARR = [T.sem.arr0, T.sem.arr1, T.sem.arr2, T.sem.arr3]
+    LD = [T.sem.ld0, T.sem.ld1, T.sem.ld2, T.sem.ld3, T.sem.ld4, T.sem.ld5, T.sem.ld6, T.sem.ld7]
+    ARR = [T.sem.arr0, T.sem.arr1, T.sem.arr2, T.sem.arr3, T.sem.arr4, T.sem.arr5, T.sem.arr6, T.sem.arr7]
     root = T.cores[12]
     rl = root % 8
     hb = root - rl
@@ -58,7 +60,8 @@ def rank_program(g, core, T, topo):
                         lands[k] += ne
     sent = 0
     for k in range(K):
-        g.dma_start(T.xs[8 * k:8 * (k + 1)], T.x[R * k:R * (k + 1), :]).then_inc(LD[k], 16)
+        q = g.sync if k % 2 == 0 else g.scalar
+        q.dma_start(T.xs[8 * k:8 * (k + 1)], T.x[R * k:R * (k + 1), :]).then_inc(LD[k], 16)
     have = 0
     for call in plan(core):
         while have <= max((p[0] for p in call)):
@@ -68,8 +71,9 @@ def rank_program(g, core, T, topo):
         sent += 16
     if core == root:
         for k in range(K):
-            g.wait_ge(ARR[k], 7 * 16 + 8)
-            g.dma_start(T.y[R * k:R * (k + 1), :], T.rb[NS * k:NS * k + 8]).then_inc(T.sem.fin, 16)
+            q = g.sync if k % 2 == 0 else g.scalar
+            q.wait_ge(ARR[k], 7 * 16 + 8)
+            q.dma_start(T.y[R * k:R * (k + 1), :], T.rb[NS * k:NS * k + 8]).then_inc(T.sem.fin, 16)
         g.wait_ge(T.sem.fin, 16 * K)
         g.wait_ge(T.sem.sent, sent)
         return

@@ -1,9 +1,9 @@
 from concourse.bass import DstId, RemoteDMATransfer
-K = 4
+K = 8
 R = 128 // K
 W = 2 * R
-NS = 15
-SCRATCH = {'xs': ('dram', [8 * K, 128, W], 'float32'), 'rb': ('dram', [NS * K, 128, W], 'float32')}
+NB = (8 * K + 6) // 7
+SCRATCH = {'xs': ('dram', [8 * K, 128, W], 'float32'), 'rb': ('dram', [8 * NB, 128, W], 'float32')}
 SEMAPHORES = ['ld0', 'ld1', 'ld2', 'ld3', 'ld4', 'ld5', 'ld6', 'ld7',
               'arr0', 'arr1', 'arr2', 'arr3', 'arr4', 'arr5', 'arr6', 'arr7', 'sent', 'fin']
 
@@ -19,74 +19,63 @@ def rank_program(g, core, T, topo):
     ha = min((c - c % 8 for c in T.cores if c - c % 8 != hb))
     loc = core % 8
     on_a = core - loc == ha
+    owners_b = [hb + i for i in range(8) if i != rl]
 
-    def owner_a(k, s):
-        if s // 4 == rl // 4:
-            return ha + 4 * (s // 4) + (s % 4 + k) % 4
-        return ha + s
+    def owner_b(j):
+        return owners_b[j % 7]
 
     def dst_id(d):
         rid, pid = topo.addr(d, core)
         return DstId(rid=rid, pnc=pid)
 
-    def plan(q):
-        ql, qa = (q % 8, q - q % 8 == ha)
-        pieces = []
-        for k in range(K):
-            for s in range(8):
-                d = owner_a(k, s) if qa or s == rl else hb + s
-                if d == q:
-                    continue
-                if qa:
-                    idx = (ql - d % 8 - 1) % 8
-                elif s == rl:
-                    idx = 7 + ql
-                else:
-                    idx = [j for j in range(8) if j != d % 8].index(ql)
-                pieces.append((k, s, d, idx))
-        calls = []
-        for i in range(0, len(pieces), 8):
-            grp = pieces[i:i + 8]
-            ne = 16 // len(grp)
-            grp = sorted(grp, key=lambda p: p[2] - p[2] % 8 == q - ql)
-            calls.append([p + ((1 << ne) - 1 << ne * j, ne) for j, p in enumerate(grp)])
-        return calls
-    lands = [0] * K
-    for q in T.cores:
-        if q != core:
-            for call in plan(q):
-                for k, s, d, idx, mask, ne in call:
-                    if d == core:
-                        lands[k] += ne
+    def peer(d):
+        return [i for i in range(8) if i != d % 8].index(loc)
+
     sent = 0
     for k in range(K):
         q = g.sync if k % 2 == 0 else g.scalar
         q.dma_start(T.xs[8 * k:8 * (k + 1)], T.x[R * k:R * (k + 1), :]).then_inc(LD[k], 16)
-    have = 0
-    for call in plan(core):
-        while have <= max((p[0] for p in call)):
-            g.wait_ge(LD[have], 16)
-            have += 1
-        g.remote_dma_fused([RemoteDMATransfer(dst_ids=[dst_id(d)], dma_engine_mask=mask, remote_sem=ARR[k], src=T.xs[8 * k + s], dst=T.rb[NS * k + idx]) for k, s, d, idx, mask, ne in call], local_sem=T.sem.sent)
-        sent += 16
+    for k in range(K):
+        g.wait_ge(LD[k], 16)
+        trs = []
+        for s in range(8):
+            j = 8 * k + s
+            d = ha + s if on_a else owner_b(j)
+            if d == core:
+                continue
+            i = len(trs)
+            if on_a:
+                mask, ne, slot = 1 << (8 + (i + k) % 8), 1, 8 * k + peer(d)
+            else:
+                mask, ne, slot = 3 << (2 * i), 2, 8 * (j // 7) + peer(d)
+            trs.append(RemoteDMATransfer(dst_ids=[dst_id(d)], dma_engine_mask=mask, remote_sem=ARR[k],
+                                         src=T.xs[j], dst=T.rb[slot]))
+            sent += ne
+        g.remote_dma_fused(trs, local_sem=T.sem.sent)
     if core == root:
         for k in range(K):
             q = g.sync if k % 2 == 0 else g.scalar
-            q.wait_ge(ARR[k], 7 * 16 + 8)
-            q.dma_start(T.y[R * k:R * (k + 1), :], T.rb[NS * k:NS * k + 8]).then_inc(T.sem.fin, 16)
+            q.wait_ge(ARR[k], 7 * 16)
+            q.dma_start(T.y[R * k:R * (k + 1), :], T.rb[8 * k:8 * (k + 1)]).then_inc(T.sem.fin, 16)
         g.wait_ge(T.sem.fin, 16 * K)
         g.wait_ge(T.sem.sent, sent)
         return
     for k in range(K):
         if on_a:
-            s = [t for t in range(8) if owner_a(k, t) == core][0]
-            n = 15 if s == rl else 7
-            g.wait_ge(ARR[k], lands[k])
-            d, out, mask, ne = (root, T.rb[NS * k + s], 255, 8) if s == rl else (hb + s, T.rb[NS * k + 7], 255, 8)
+            j = 8 * k + loc
+            g.wait_ge(ARR[k], 7)
+            trs = [RemoteDMATransfer(dst_ids=[dst_id(owner_b(j))], dma_engine_mask=255, remote_sem=ARR[k],
+                                     srcs=[T.xs[j]] + [T.rb[8 * k + i] for i in range(7)],
+                                     dsts=[T.rb[8 * (j // 7) + 7]], alu_op=1)]
+            sent += 8
         else:
-            s, n = (loc, 8)
-            g.wait_ge(ARR[k], lands[k] + 8)
-            d, out, mask, ne = (root, T.rb[NS * k + s], 65535, 16)
-        g.remote_dma_fused([RemoteDMATransfer(dst_ids=[dst_id(d)], dma_engine_mask=mask, remote_sem=ARR[k], srcs=[T.xs[8 * k + s]] + [T.rb[NS * k + i] for i in range(n)], dsts=[out], alu_op=1)], local_sem=T.sem.sent)
-        sent += ne
+            mine = [j for j in range(8 * k, 8 * k + 8) if owner_b(j) == core]
+            g.wait_ge(ARR[k], len(mine) * (7 * 2 + 8))
+            ne = 16 // len(mine)
+            trs = [RemoteDMATransfer(dst_ids=[dst_id(root)], dma_engine_mask=((1 << ne) - 1) << (ne * t),
+                                     remote_sem=ARR[k],
+                                     srcs=[T.xs[j]] + [T.rb[8 * (j // 7) + i] for i in range(8)],
+                                     dsts=[T.rb[j]], alu_op=1) for t, j in enumerate(mine)]
+            sent += 16
+        g.remote_dma_fused(trs, local_sem=T.sem.sent)
     g.wait_ge(T.sem.sent, sent)

@@ -1,9 +1,13 @@
 from concourse.bass import DstId, RemoteDMATransfer
-K = 8
-R = 128 // K
-W = 2 * R
-NB = (8 * K + 6) // 7
-SCRATCH = {'xs': ('dram', [8 * K, 128, W], 'float32'), 'rb': ('dram', [8 * NB, 128, W], 'float32')}
+ROWS = [8, 24, 32, 32, 24, 8]
+WIDE = 3
+K = len(ROWS)
+OFF = [sum(ROWS[:k]) for k in range(K + 1)]
+SCRATCH = {}
+for _k in range(8):
+    _w = 2 * ROWS[_k] if _k < K else 2
+    SCRATCH['xs%d' % _k] = ('dram', [8 if _k < K else 1, 128, _w], 'float32')
+    SCRATCH['rb%d' % _k] = ('dram', [16 if _k < K else 1, 128, _w], 'float32')
 SEMAPHORES = ['ld0', 'ld1', 'ld2', 'ld3', 'ld4', 'ld5', 'ld6', 'ld7',
               'arr0', 'arr1', 'arr2', 'arr3', 'arr4', 'arr5', 'arr6', 'arr7', 'sent', 'fin']
 
@@ -13,6 +17,8 @@ def rank_program(g, core, T, topo):
         return
     LD = [T.sem.ld0, T.sem.ld1, T.sem.ld2, T.sem.ld3, T.sem.ld4, T.sem.ld5, T.sem.ld6, T.sem.ld7]
     ARR = [T.sem.arr0, T.sem.arr1, T.sem.arr2, T.sem.arr3, T.sem.arr4, T.sem.arr5, T.sem.arr6, T.sem.arr7]
+    XS = [T.xs0, T.xs1, T.xs2, T.xs3, T.xs4, T.xs5, T.xs6, T.xs7]
+    RB = [T.rb0, T.rb1, T.rb2, T.rb3, T.rb4, T.rb5, T.rb6, T.rb7]
     root = T.cores[12]
     rl = root % 8
     hb = root - rl
@@ -21,8 +27,11 @@ def rank_program(g, core, T, topo):
     on_a = core - loc == ha
     owners_b = [hb + i for i in range(8) if i != rl]
 
-    def owner_b(j):
-        return owners_b[j % 7]
+    def owner_b(k, s):
+        return owners_b[(8 * k + s) % 7]
+
+    def base_b(k, s):
+        return 8 * len([t for t in range(s) if owner_b(k, t) == owner_b(k, s)])
 
     def dst_id(d):
         rid, pid = topo.addr(d, core)
@@ -34,48 +43,48 @@ def rank_program(g, core, T, topo):
     sent = 0
     for k in range(K):
         q = g.sync if k % 2 == 0 else g.scalar
-        q.dma_start(T.xs[8 * k:8 * (k + 1)], T.x[R * k:R * (k + 1), :]).then_inc(LD[k], 16)
+        q.dma_start(XS[k][:], T.x[OFF[k]:OFF[k + 1], :]).then_inc(LD[k], 16)
     for k in range(K):
         g.wait_ge(LD[k], 16)
         trs = []
         for s in range(8):
-            j = 8 * k + s
-            d = ha + s if on_a else owner_b(j)
+            d = ha + s if on_a else owner_b(k, s)
             if d == core:
                 continue
             i = len(trs)
-            if on_a:
-                mask, ne, slot = 1 << (8 + (i + k) % 8), 1, 8 * k + peer(d)
+            if on_a and k >= WIDE:
+                mask, ne, slot = 1 << (8 + (i + k) % 8), 1, peer(d)
+            elif on_a:
+                mask, ne, slot = 3 << (2 * i + 2), 2, peer(d)
             else:
-                mask, ne, slot = 3 << (2 * i), 2, 8 * (j // 7) + peer(d)
+                mask, ne, slot = 3 << (2 * i), 2, base_b(k, s) + peer(d)
             trs.append(RemoteDMATransfer(dst_ids=[dst_id(d)], dma_engine_mask=mask, remote_sem=ARR[k],
-                                         src=T.xs[j], dst=T.rb[slot]))
+                                         src=XS[k][s], dst=RB[k][slot]))
             sent += ne
         g.remote_dma_fused(trs, local_sem=T.sem.sent)
     if core == root:
         for k in range(K):
             q = g.sync if k % 2 == 0 else g.scalar
             q.wait_ge(ARR[k], 7 * 16)
-            q.dma_start(T.y[R * k:R * (k + 1), :], T.rb[8 * k:8 * (k + 1)]).then_inc(T.sem.fin, 16)
+            q.dma_start(T.y[OFF[k]:OFF[k + 1], :], RB[k][0:8]).then_inc(T.sem.fin, 16)
         g.wait_ge(T.sem.fin, 16 * K)
         g.wait_ge(T.sem.sent, sent)
         return
     for k in range(K):
         if on_a:
-            j = 8 * k + loc
-            g.wait_ge(ARR[k], 7)
-            trs = [RemoteDMATransfer(dst_ids=[dst_id(owner_b(j))], dma_engine_mask=255, remote_sem=ARR[k],
-                                     srcs=[T.xs[j]] + [T.rb[8 * k + i] for i in range(7)],
-                                     dsts=[T.rb[8 * (j // 7) + 7]], alu_op=1)]
+            g.wait_ge(ARR[k], 7 * (2 if k < WIDE else 1))
+            trs = [RemoteDMATransfer(dst_ids=[dst_id(owner_b(k, loc))], dma_engine_mask=255, remote_sem=ARR[k],
+                                     srcs=[XS[k][loc]] + [RB[k][i] for i in range(7)],
+                                     dsts=[RB[k][base_b(k, loc) + 7]], alu_op=1)]
             sent += 8
         else:
-            mine = [j for j in range(8 * k, 8 * k + 8) if owner_b(j) == core]
+            mine = [s for s in range(8) if owner_b(k, s) == core]
             g.wait_ge(ARR[k], len(mine) * (7 * 2 + 8))
             ne = 16 // len(mine)
             trs = [RemoteDMATransfer(dst_ids=[dst_id(root)], dma_engine_mask=((1 << ne) - 1) << (ne * t),
                                      remote_sem=ARR[k],
-                                     srcs=[T.xs[j]] + [T.rb[8 * (j // 7) + i] for i in range(8)],
-                                     dsts=[T.rb[j]], alu_op=1) for t, j in enumerate(mine)]
+                                     srcs=[XS[k][s]] + [RB[k][base_b(k, s) + i] for i in range(8)],
+                                     dsts=[RB[k][s]], alu_op=1) for t, s in enumerate(mine)]
             sent += 16
         g.remote_dma_fused(trs, local_sem=T.sem.sent)
     g.wait_ge(T.sem.sent, sent)

@@ -1,5 +1,5 @@
 from concourse.bass import DstId, RemoteDMATransfer
-ROWS = [8, 24, 32, 32, 24, 8]
+ROWS = [8, 24, 24, 24, 24, 16, 8]
 WIDE = 3
 K = len(ROWS)
 OFF = [sum(ROWS[:k]) for k in range(K + 1)]
@@ -26,6 +26,7 @@ def rank_program(g, core, T, topo):
     loc = core % 8
     on_a = core - loc == ha
     owners_b = [hb + i for i in range(8) if i != rl]
+    sent = [0]
 
     def owner_b(k, s):
         return owners_b[(8 * k + s) % 7]
@@ -40,11 +41,7 @@ def rank_program(g, core, T, topo):
     def peer(d):
         return [i for i in range(8) if i != d % 8].index(loc)
 
-    sent = 0
-    for k in range(K):
-        q = g.sync if k % 2 == 0 else g.scalar
-        q.dma_start(XS[k][:], T.x[OFF[k]:OFF[k + 1], :]).then_inc(LD[k], 16)
-    for k in range(K):
+    def scatter(k):
         g.wait_ge(LD[k], 16)
         trs = []
         for s in range(8):
@@ -60,23 +57,16 @@ def rank_program(g, core, T, topo):
                 mask, ne, slot = 3 << (2 * i), 2, base_b(k, s) + peer(d)
             trs.append(RemoteDMATransfer(dst_ids=[dst_id(d)], dma_engine_mask=mask, remote_sem=ARR[k],
                                          src=XS[k][s], dst=RB[k][slot]))
-            sent += ne
+            sent[0] += ne
         g.remote_dma_fused(trs, local_sem=T.sem.sent)
-    if core == root:
-        for k in range(K):
-            q = g.sync if k % 2 == 0 else g.scalar
-            q.wait_ge(ARR[k], 7 * 16)
-            q.dma_start(T.y[OFF[k]:OFF[k + 1], :], RB[k][0:8]).then_inc(T.sem.fin, 16)
-        g.wait_ge(T.sem.fin, 16 * K)
-        g.wait_ge(T.sem.sent, sent)
-        return
-    for k in range(K):
+
+    def fold(k):
         if on_a:
             g.wait_ge(ARR[k], 7 * (2 if k < WIDE else 1))
             trs = [RemoteDMATransfer(dst_ids=[dst_id(owner_b(k, loc))], dma_engine_mask=255, remote_sem=ARR[k],
                                      srcs=[XS[k][loc]] + [RB[k][i] for i in range(7)],
                                      dsts=[RB[k][base_b(k, loc) + 7]], alu_op=1)]
-            sent += 8
+            sent[0] += 8
         else:
             mine = [s for s in range(8) if owner_b(k, s) == core]
             g.wait_ge(ARR[k], len(mine) * (7 * 2 + 8))
@@ -85,6 +75,22 @@ def rank_program(g, core, T, topo):
                                      remote_sem=ARR[k],
                                      srcs=[XS[k][s]] + [RB[k][base_b(k, s) + i] for i in range(8)],
                                      dsts=[RB[k][s]], alu_op=1) for t, s in enumerate(mine)]
-            sent += 16
+            sent[0] += 16
         g.remote_dma_fused(trs, local_sem=T.sem.sent)
-    g.wait_ge(T.sem.sent, sent)
+
+    for k in range(K):
+        q = g.sync if k % 2 == 0 else g.scalar
+        q.dma_start(XS[k][:], T.x[OFF[k]:OFF[k + 1], :]).then_inc(LD[k], 16)
+    for k in range(K):
+        scatter(k)
+    if core == root:
+        for k in range(K):
+            q = g.sync if k % 2 == 0 else g.scalar
+            q.wait_ge(ARR[k], 7 * 16)
+            q.dma_start(T.y[OFF[k]:OFF[k + 1], :], RB[k][0:8]).then_inc(T.sem.fin, 16)
+        g.wait_ge(T.sem.fin, 16 * K)
+        g.wait_ge(T.sem.sent, sent[0])
+        return
+    for k in range(K):
+        fold(k)
+    g.wait_ge(T.sem.sent, sent[0])

from concourse.bass import DstId, RemoteDMATransfer
ROWS = [8, 24, 24, 24, 24, 16, 8]
WIDE = 3
K = len(ROWS)
OFF = [sum(ROWS[:k]) for k in range(K + 1)]
SCRATCH = {}
for _k in range(8):
    _w = 2 * ROWS[_k] if _k < K else 2
    SCRATCH['xs%d' % _k] = ('dram', [8 if _k < K else 1, 128, _w], 'float32')
    SCRATCH['rb%d' % _k] = ('dram', [16 if _k < K else 1, 128, _w], 'float32')
SEMAPHORES = ['ld0', 'ld1', 'ld2', 'ld3', 'ld4', 'ld5', 'ld6', 'ld7',
              'arr0', 'arr1', 'arr2', 'arr3', 'arr4', 'arr5', 'arr6', 'arr7', 'sent', 'fin']


def rank_program(g, core, T, topo):
    if T.rank_of(core) is None:
        return
    LD = [T.sem.ld0, T.sem.ld1, T.sem.ld2, T.sem.ld3, T.sem.ld4, T.sem.ld5, T.sem.ld6, T.sem.ld7]
    ARR = [T.sem.arr0, T.sem.arr1, T.sem.arr2, T.sem.arr3, T.sem.arr4, T.sem.arr5, T.sem.arr6, T.sem.arr7]
    XS = [T.xs0, T.xs1, T.xs2, T.xs3, T.xs4, T.xs5, T.xs6, T.xs7]
    RB = [T.rb0, T.rb1, T.rb2, T.rb3, T.rb4, T.rb5, T.rb6, T.rb7]
    root = T.cores[12]
    rl = root % 8
    hb = root - rl
    ha = min((c - c % 8 for c in T.cores if c - c % 8 != hb))
    loc = core % 8
    on_a = core - loc == ha
    owners_b = [hb + i for i in range(8) if i != rl]
    sent = [0]

    def owner_b(k, s):
        return owners_b[(8 * k + s) % 7]

    def base_b(k, s):
        return 8 * len([t for t in range(s) if owner_b(k, t) == owner_b(k, s)])

    def dst_id(d):
        rid, pid = topo.addr(d, core)
        return DstId(rid=rid, pnc=pid)

    def peer(d):
        return [i for i in range(8) if i != d % 8].index(loc)

    def scatter(k):
        g.wait_ge(LD[k], 16)
        trs = []
        for s in range(8):
            d = ha + s if on_a else owner_b(k, s)
            if d == core:
                continue
            i = len(trs)
            if on_a and k >= WIDE:
                mask, ne, slot = 1 << (8 + (i + k) % 8), 1, peer(d)
            elif on_a:
                mask, ne, slot = 3 << (2 * i + 2), 2, peer(d)
            else:
                mask, ne, slot = 3 << (2 * i), 2, base_b(k, s) + peer(d)
            trs.append(RemoteDMATransfer(dst_ids=[dst_id(d)], dma_engine_mask=mask, remote_sem=ARR[k],
                                         src=XS[k][s], dst=RB[k][slot]))
            sent[0] += ne
        g.remote_dma_fused(trs, local_sem=T.sem.sent)

    def fold(k):
        if on_a:
            g.wait_ge(ARR[k], 7 * (2 if k < WIDE else 1))
            trs = [RemoteDMATransfer(dst_ids=[dst_id(owner_b(k, loc))], dma_engine_mask=255, remote_sem=ARR[k],
                                     srcs=[XS[k][loc]] + [RB[k][i] for i in range(7)],
                                     dsts=[RB[k][base_b(k, loc) + 7]], alu_op=1)]
            sent[0] += 8
        else:
            mine = [s for s in range(8) if owner_b(k, s) == core]
            g.wait_ge(ARR[k], len(mine) * (7 * 2 + 8))
            ne = 16 // len(mine)
            trs = [RemoteDMATransfer(dst_ids=[dst_id(root)], dma_engine_mask=((1 << ne) - 1) << (ne * t),
                                     remote_sem=ARR[k],
                                     srcs=[XS[k][s]] + [RB[k][base_b(k, s) + i] for i in range(8)],
                                     dsts=[RB[k][s]], alu_op=1) for t, s in enumerate(mine)]
            sent[0] += 16
        g.remote_dma_fused(trs, local_sem=T.sem.sent)

    for k in range(K):
        q = g.sync if k % 2 == 0 else g.scalar
        q.dma_start(XS[k][:], T.x[OFF[k]:OFF[k + 1], :]).then_inc(LD[k], 16)
    for k in range(K):
        scatter(k)
    if core == root:
        for k in range(K):
            q = g.sync if k % 2 == 0 else g.scalar
            q.wait_ge(ARR[k], 7 * 16)
            q.dma_start(T.y[OFF[k]:OFF[k + 1], :], RB[k][0:8]).then_inc(T.sem.fin, 16)
        g.wait_ge(T.sem.fin, 16 * K)
        g.wait_ge(T.sem.sent, sent[0])
        return
    for k in range(K):
        fold(k)
    g.wait_ge(T.sem.sent, sent[0])
